import numpy as np
import ml_dtypes

BF16 = ml_dtypes.bfloat16


def bf(x):
    return np.asarray(x, np.float32).astype(BF16)


def f32(x):
    return np.asarray(x, np.float32)


def f64(x):
    return np.asarray(x).astype(np.float64)


def striped(idx):
    return np.tile(idx.reshape(-1, 16).T, (8, 1))


S, K, M, N, D, V = 512, 128, 512, 384, 4, 96


def setup_inputs():
    return {"table": bf(np.random.standard_normal((K, S))), "w": bf(np.random.standard_normal((K, M)) / np.sqrt(K)), "b": f32(0.5 * np.random.standard_normal((M, 1))), "offs": striped(np.random.permutation(np.tile(np.arange(S), 2))[:N])}


def reference(table, w, b, offs):
    idx = offs[:16].T.reshape(-1)
    x = f64(table)[:, idx]
    y = f64(w).T @ x
    z = np.tanh(y + f64(b))
    return z.reshape(M, V, D).mean(axis=2)

@@ -1,0 +1,47 @@
+import concourse.mybir as mybir
+
+BF16, F32, U16 = mybir.dt.bfloat16, mybir.dt.float32, mybir.dt.uint16
+TANH = mybir.ActivationFunctionType.Tanh
+ADD = mybir.AluOpType.add
+X = mybir.AxisListType.X
+
+P = 128
+S = 512
+M = 512
+N = 384
+D = 4
+V = N // D
+
+FLOPS = 2 * P * M * N
+
+
+def tile_gather_matmul_kernel(tc, table, w, b, offs, out):
+    nc = tc.nc
+    blocks = M // P
+    with (
+        tc.tile_pool(name="held", bufs=1) as held,
+        tc.tile_pool(name="work", bufs=2) as work,
+        tc.psum_pool(name="psum", bufs=blocks) as psum,
+    ):
+        offsets = held.tile([P, N // 16], U16, name="offsets")
+        nc.sync.dma_start(offsets[:], offs)
+        nodes = held.tile([P, S], BF16, name="nodes")
+        nc.sync.dma_start(nodes[:], table)
+        weights = held.tile([P, M], BF16, name="weights")
+        nc.scalar.dma_start(weights[:], w)
+        bias = held.tile([P, blocks], F32, name="bias")
+        nc.scalar.dma_start(bias[:], b.rearrange("(a p) o -> p (a o)", p=P))
+
+        for a in range(blocks):
+            y = psum.tile([P, N], F32, name="y")
+            nc.tensor.matmul(
+                y[:], weights[:, a * P : (a + 1) * P], nodes[:].indirect(offsets[:]),
+                start=True, stop=True,
+            )
+            z = work.tile([P, N], F32, name="z")
+            nc.scalar.activation(z[:], y[:], TANH, bias=bias[:, a : a + 1])
+            total = work.tile([P, V], F32, name="total")
+            nc.vector.tensor_reduce(total[:], z[:].rearrange("p (v t) -> p v t", t=D), axis=X, op=ADD)
+            mean = work.tile([P, V], F32, name="mean")
+            nc.vector.tensor_scalar_mul(mean[:], total[:], 1.0 / D)
+            nc.sync.dma_start(out[a * P : (a + 1) * P, :], mean[:])

@@ -32,6 +32,11 @@ def tile_gather_matmul_kernel(tc, table, w, b, offs, out):
         bias = held.tile([P, blocks], F32, name="bias")
         nc.scalar.dma_start(bias[:], b.rearrange("(a p) o -> p (a o)", p=P))
 
+        early = held.tile([P, 1], F32, name="early")
+        nc.vector.memset(early[:], 0.0)
+        early_tanh = held.tile([P, 1], F32, name="early_tanh")
+        nc.scalar.activation(early_tanh[:], early[:], TANH)
+
         for a in range(blocks):
             y = psum.tile([P, N], F32, name="y")
             nc.tensor.matmul(

@@ -20,7 +20,7 @@ def tile_gather_matmul_kernel(tc, table, w, b, offs, out):
     blocks = M // P
     with (
         tc.tile_pool(name="held", bufs=1) as held,
-        tc.tile_pool(name="work", bufs=2) as work,
+        tc.tile_pool(name="work", bufs=blocks) as work,
         tc.psum_pool(name="psum", bufs=blocks) as psum,
     ):
         offsets = held.tile([P, N // 16], U16, name="offsets")
@@ -30,7 +30,9 @@ def tile_gather_matmul_kernel(tc, table, w, b, offs, out):
         weights = held.tile([P, M], BF16, name="weights")
         nc.scalar.dma_start(weights[:], w)
         bias = held.tile([P, blocks], F32, name="bias")
-        nc.scalar.dma_start(bias[:], b.rearrange("(a p) o -> p (a o)", p=P))
+        nc.scalar.dma_start(bias[:], b.rearrange("(p a) o -> p (a o)", a=blocks))
+        weight_block = weights[:].rearrange("k (p a) -> k p a", a=blocks)
+        out_block = out.rearrange("(p a) v -> p a v", a=blocks)
 
         early = held.tile([P, 1], F32, name="early")
         nc.vector.memset(early[:], 0.0)
@@ -40,7 +42,7 @@ def tile_gather_matmul_kernel(tc, table, w, b, offs, out):
         for a in range(blocks):
             y = psum.tile([P, N], F32, name="y")
             nc.tensor.matmul(
-                y[:], weights[:, a * P : (a + 1) * P], nodes[:].indirect(offsets[:]),
+                y[:], weight_block[:, :, a], nodes[:].indirect(offsets[:]),
                 start=True, stop=True,
             )
             z = work.tile([P, N], F32, name="z")
@@ -49,4 +51,4 @@ def tile_gather_matmul_kernel(tc, table, w, b, offs, out):
             nc.vector.tensor_reduce(total[:], z[:].rearrange("p (v t) -> p v t", t=D), axis=X, op=ADD)
             mean = work.tile([P, V], F32, name="mean")
             nc.vector.tensor_scalar_mul(mean[:], total[:], 1.0 / D)
-            nc.sync.dma_start(out[a * P : (a + 1) * P, :], mean[:])
+            nc.sync.dma_start(out_block[:, a, :], mean[:])

@@ -12,6 +12,8 @@ N = 384
 D = 4
 V = N // D
 
+WARM_UPS, WARM_UP_COLUMNS = 8, 256
+
 FLOPS = 2 * P * M * N
 
 
@@ -22,6 +24,7 @@ def tile_gather_matmul_kernel(tc, table, w, b, offs, out):
         tc.tile_pool(name="held", bufs=1) as held,
         tc.tile_pool(name="work", bufs=blocks) as work,
         tc.psum_pool(name="psum", bufs=blocks) as psum,
+        tc.psum_pool(name="scratch", bufs=1) as scratch,
     ):
         offsets = held.tile([P, N // 16], U16, name="offsets")
         nc.sync.dma_start(offsets[:], offs)
@@ -34,10 +37,13 @@ def tile_gather_matmul_kernel(tc, table, w, b, offs, out):
         weight_block = weights[:].rearrange("k (p a) -> k p a", a=blocks)
         out_block = out.rearrange("(p a) v -> p a v", a=blocks)
 
-        early = held.tile([P, 1], F32, name="early")
-        nc.vector.memset(early[:], 0.0)
+        zeros = held.tile([P, WARM_UP_COLUMNS], BF16, name="zeros")
+        nc.vector.memset(zeros[:], 0.0)
+        scrap = scratch.tile([P, WARM_UP_COLUMNS], F32, name="scrap")
+        for i in range(WARM_UPS):
+            nc.tensor.matmul(scrap[:], zeros[:, 0:P], zeros[:], start=True, stop=True)
         early_tanh = held.tile([P, 1], F32, name="early_tanh")
-        nc.scalar.activation(early_tanh[:], early[:], TANH)
+        nc.scalar.activation(early_tanh[:], zeros[:, 0:1], TANH)
 
         for a in range(blocks):
             y = psum.tile([P, N], F32, name="y")

@@ -11,8 +11,7 @@ M = 512
 N = 384
 D = 4
 V = N // D
-
-WARM_UPS, WARM_UP_COLUMNS = 8, 256
+HALVES = 2
 
 FLOPS = 2 * P * M * N
 
@@ -24,7 +23,6 @@ def tile_gather_matmul_kernel(tc, table, w, b, offs, out):
         tc.tile_pool(name="held", bufs=1) as held,
         tc.tile_pool(name="work", bufs=blocks) as work,
         tc.psum_pool(name="psum", bufs=blocks) as psum,
-        tc.psum_pool(name="scratch", bufs=1) as scratch,
     ):
         offsets = held.tile([P, N // 16], U16, name="offsets")
         nc.sync.dma_start(offsets[:], offs)
@@ -37,24 +35,31 @@ def tile_gather_matmul_kernel(tc, table, w, b, offs, out):
         weight_block = weights[:].rearrange("k (p a) -> k p a", a=blocks)
         out_block = out.rearrange("(p a) v -> p a v", a=blocks)
 
-        zeros = held.tile([P, WARM_UP_COLUMNS], BF16, name="zeros")
-        nc.vector.memset(zeros[:], 0.0)
-        scrap = scratch.tile([P, WARM_UP_COLUMNS], F32, name="scrap")
-        for i in range(WARM_UPS):
-            nc.tensor.matmul(scrap[:], zeros[:, 0:P], zeros[:], start=True, stop=True)
+        early = held.tile([P, 1], F32, name="early")
+        nc.vector.memset(early[:], 0.0)
         early_tanh = held.tile([P, 1], F32, name="early_tanh")
-        nc.scalar.activation(early_tanh[:], zeros[:, 0:1], TANH)
+        nc.scalar.activation(early_tanh[:], early[:], TANH)
 
+        sums = held.tile([P, blocks, V], F32, name="sums")
         for a in range(blocks):
             y = psum.tile([P, N], F32, name="y")
-            nc.tensor.matmul(
-                y[:], weight_block[:, :, a], nodes[:].indirect(offsets[:]),
-                start=True, stop=True,
-            )
             z = work.tile([P, N], F32, name="z")
-            nc.scalar.activation(z[:], y[:], TANH, bias=bias[:, a : a + 1])
-            total = work.tile([P, V], F32, name="total")
-            nc.vector.tensor_reduce(total[:], z[:].rearrange("p (v t) -> p v t", t=D), axis=X, op=ADD)
-            mean = work.tile([P, V], F32, name="mean")
-            nc.vector.tensor_scalar_mul(mean[:], total[:], 1.0 / D)
-            nc.sync.dma_start(out_block[:, a, :], mean[:])
+            for h in range(HALVES):
+                entries = slice(h * N // HALVES, (h + 1) * N // HALVES)
+                offset_columns = slice(h * N // 16 // HALVES, (h + 1) * N // 16 // HALVES)
+                pooled = slice(h * V // HALVES, (h + 1) * V // HALVES)
+                nc.tensor.matmul(
+                    y[:, entries], weight_block[:, :, a], nodes[:].indirect(offsets[:, offset_columns]),
+                    start=True, stop=True,
+                )
+                nc.scalar.activation(z[:, entries], y[:, entries], TANH, bias=bias[:, a : a + 1])
+                neighbours = z[:, entries].rearrange("p (v t) -> p v t", t=D)
+                nc.vector.tensor_reduce(sums[:, a, pooled], neighbours, axis=X, op=ADD)
+
+        half = blocks // 2
+        first_means = held.tile([P, half, V], F32, name="first_means")
+        nc.scalar.mul(first_means[:], sums[:, 0:half, :], 1.0 / D)
+        nc.sync.dma_start(out_block[:, 0:half, :], first_means[:])
+        second_means = held.tile([P, half, V], F32, name="second_means")
+        nc.vector.tensor_scalar_mul(second_means[:], sums[:, half:blocks, :], 1.0 / D)
+        nc.sync.dma_start(out_block[:, half:blocks, :], second_means[:])

import concourse.mybir as mybir

BF16, F32, U16 = mybir.dt.bfloat16, mybir.dt.float32, mybir.dt.uint16
TANH = mybir.ActivationFunctionType.Tanh
ADD = mybir.AluOpType.add
X = mybir.AxisListType.X

P = 128
S = 512
M = 512
N = 384
D = 4
V = N // D
HALVES = 2

FLOPS = 2 * P * M * N


def tile_gather_matmul_kernel(tc, table, w, b, offs, out):
    nc = tc.nc
    blocks = M // P
    with (
        tc.tile_pool(name="held", bufs=1) as held,
        tc.tile_pool(name="work", bufs=blocks) as work,
        tc.psum_pool(name="psum", bufs=blocks) as psum,
    ):
        offsets = held.tile([P, N // 16], U16, name="offsets")
        nc.sync.dma_start(offsets[:], offs)
        nodes = held.tile([P, S], BF16, name="nodes")
        nc.sync.dma_start(nodes[:], table)
        weights = held.tile([P, M], BF16, name="weights")
        nc.scalar.dma_start(weights[:], w)
        bias = held.tile([P, blocks], F32, name="bias")
        nc.scalar.dma_start(bias[:], b.rearrange("(p a) o -> p (a o)", a=blocks))
        weight_block = weights[:].rearrange("k (p a) -> k p a", a=blocks)
        out_block = out.rearrange("(p a) v -> p a v", a=blocks)

        early = held.tile([P, 1], F32, name="early")
        nc.vector.memset(early[:], 0.0)
        early_tanh = held.tile([P, 1], F32, name="early_tanh")
        nc.scalar.activation(early_tanh[:], early[:], TANH)

        sums = held.tile([P, blocks, V], F32, name="sums")
        for a in range(blocks):
            y = psum.tile([P, N], F32, name="y")
            z = work.tile([P, N], F32, name="z")
            for h in range(HALVES):
                entries = slice(h * N // HALVES, (h + 1) * N // HALVES)
                offset_columns = slice(h * N // 16 // HALVES, (h + 1) * N // 16 // HALVES)
                pooled = slice(h * V // HALVES, (h + 1) * V // HALVES)
                nc.tensor.matmul(
                    y[:, entries], weight_block[:, :, a], nodes[:].indirect(offsets[:, offset_columns]),
                    start=True, stop=True,
                )
                nc.scalar.activation(z[:, entries], y[:, entries], TANH, bias=bias[:, a : a + 1])
                neighbours = z[:, entries].rearrange("p (v t) -> p v t", t=D)
                nc.vector.tensor_reduce(sums[:, a, pooled], neighbours, axis=X, op=ADD)

        half = blocks // 2
        first_means = held.tile([P, half, V], F32, name="first_means")
        nc.scalar.mul(first_means[:], sums[:, 0:half, :], 1.0 / D)
        nc.sync.dma_start(out_block[:, 0:half, :], first_means[:])
        second_means = held.tile([P, half, V], F32, name="second_means")
        nc.vector.tensor_scalar_mul(second_means[:], sums[:, half:blocks, :], 1.0 / D)
        nc.sync.dma_start(out_block[:, half:blocks, :], second_means[:])
